import numpy as np
CORES = [50,51,178,179,306,307,434,435]
N = 8
def setup_inputs(rng):
    return {"x": rng.standard_normal((N, 128, 64), dtype=np.float32)}
def reference(x):
    g = np.ascontiguousarray(x.transpose(1, 2, 0)).reshape(128, 64 * N)
    return {"y": np.broadcast_to(g, (N,) + g.shape)}

@@ -1,0 +1,100 @@
+from concourse.bass import DstId, RemoteDMATransfer
+
+CHIPS = [6]
+C = len(CHIPS)
+W = 16 * C
+K = 128 // W
+M = K // 2
+
+SCRATCH = {
+    "xs": ("dram", [W, 128, M], "float32"),
+    "inp": ("dram", [8, 128, M], "float32"),
+    "il": ("dram", [128, 8 * M], "float32"),
+    "yq": ("dram", [W, 128, 8 * M], "float32"),
+}
+SEMAPHORES = ["load", "near", "far", "wove", "res", "own", "out", "sent"]
+
+POS = {0: 0, 3: 0, 1: 1, 2: 1}
+HOST_AT = {(0, 0): 0, (0, 1): 1, (1, 0): 3, (1, 1): 2}
+
+
+def worker_core(rack, b):
+    pos, rest = divmod(b, 8 * C)
+    ci, d = divmod(rest, 8)
+    return HOST_AT[(rack, pos)] * 128 + CHIPS[ci] * 8 + d
+
+
+def rank_program(g, core, T, topo):
+    host, chip, d = topo.host(core), topo.chip(core), core % 8
+    if chip not in CHIPS:
+        return
+    rack = topo.rack(host)
+    rank = T.rank_of(core)
+    b = (POS[host] * C + CHIPS.index(chip)) * 8 + d
+    S = T.sem
+    sent = 0
+
+    def did(dst):
+        rid, pid = topo.addr(dst, core)
+        return DstId(rid=rid, pnc=pid)
+
+    def on_chip(dst):
+        return dst // 8 == core // 8
+
+    if rank is not None:
+        g.sync.dma_start(T.xs[:], T.x[:]).then_inc(S.load, 16)
+        g.wait_ge(S.load, 16)
+        near_in = [w for w in range(W) if on_chip(worker_core(rack, w)) and w != b]
+        near_off = [w for w in range(W) if not on_chip(worker_core(rack, w))]
+        while near_in or near_off:
+            trs = []
+            for e in range(8):
+                if near_off:
+                    w = near_off.pop(0)
+                    trs.append(RemoteDMATransfer(dst_ids=[did(worker_core(rack, w))], dma_engine_mask=1 << e,
+                                                 remote_sem=S.near, src=T.xs[w], dst=T.inp[rank]))
+                if near_in:
+                    w = near_in.pop(0)
+                    trs.append(RemoteDMATransfer(dst_ids=[did(worker_core(rack, w))], dma_engine_mask=1 << (8 + e),
+                                                 remote_sem=S.near, src=T.xs[w], dst=T.inp[rank]))
+            g.remote_dma_fused(trs, local_sem=S.sent)
+            sent += len(trs)
+
+    def piece(r):
+        return T.xs[b] if r == rank else T.inp[r]
+
+    near = [4 * rack + q for q in range(4)]
+    far = [4 * (1 - rack) + q for q in range(4)]
+
+    g.wait_ge(S.near, 3 if rank is not None else 4)
+    mate = did((3 - host) * 128 + chip * 8 + d)
+    g.remote_dma_fused([RemoteDMATransfer(dst_ids=[mate], dma_engine_mask=3 << (2 * q), remote_sem=S.far,
+                                          src=piece(r), dst=T.inp[r]) for q, r in enumerate(near)],
+                       local_sem=S.sent)
+    sent += 8
+
+    for r in near:
+        g.dma_start(T.il[:, r::8], piece(r), allow_slow_non_contiguous=True).then_inc(S.wove, 16)
+    g.wait_ge(S.far, 8)
+    for r in far:
+        g.dma_start(T.il[:, r::8], piece(r), allow_slow_non_contiguous=True).then_inc(S.wove, 16)
+    g.wait_ge(S.wove, 128)
+
+    dsts = [T.cores[r] for r in near if r != rank]
+    trs = []
+    for mask, grp in ((0xFF00, [c for c in dsts if on_chip(c)]), (0x00FF, [c for c in dsts if not on_chip(c)])):
+        if grp:
+            trs.append(RemoteDMATransfer(dst_ids=[did(c) for c in grp], dma_engine_mask=mask, remote_sem=S.res,
+                                         srcs=[T.il[:]], dsts=[T.yq[b] for c in grp]))
+            sent += 8
+    g.remote_dma_fused(trs, local_sem=S.sent)
+
+    if rank is not None:
+        g.dma_start(T.y[b * K:(b + 1) * K, :], T.il[:]).then_inc(S.own, 16)
+        g.sync.wait_ge(S.res, 8 * (W - 1))
+        g.sync.dma_start(T.y[0:b * K, :], T.yq[0:b]).then_inc(S.out, 16)
+        g.scalar.wait_ge(S.res, 8 * (W - 1))
+        g.scalar.dma_start(T.y[(b + 1) * K:, :], T.yq[b + 1:]).then_inc(S.out, 16)
+        g.wait_ge(S.own, 16)
+        g.wait_ge(S.out, 32)
+    g.wait_ge(S.sent, sent)

@@ -12,7 +12,7 @@ SCRATCH = {
     "il": ("dram", [128, 8 * M], "float32"),
     "yq": ("dram", [W, 128, 8 * M], "float32"),
 }
-SEMAPHORES = ["load", "near", "far", "wove", "res", "own", "out", "sent"]
+SEMAPHORES = ["load", "near", "far", "wove", "resin", "resoff", "own", "out", "sent"]
 
 POS = {0: 0, 3: 0, 1: 1, 2: 1}
 HOST_AT = {(0, 0): 0, (0, 1): 1, (1, 0): 3, (1, 1): 2}
@@ -82,19 +82,23 @@ def rank_program(g, core, T, topo):
 
     dsts = [T.cores[r] for r in near if r != rank]
     trs = []
-    for mask, grp in ((0xFF00, [c for c in dsts if on_chip(c)]), (0x00FF, [c for c in dsts if not on_chip(c)])):
+    for mask, sem, grp in ((0x00FF, S.resoff, [c for c in dsts if not on_chip(c)]),
+                           (0xFF00, S.resin, [c for c in dsts if on_chip(c)])):
         if grp:
-            trs.append(RemoteDMATransfer(dst_ids=[did(c) for c in grp], dma_engine_mask=mask, remote_sem=S.res,
+            trs.append(RemoteDMATransfer(dst_ids=[did(c) for c in grp], dma_engine_mask=mask, remote_sem=sem,
                                          srcs=[T.il[:]], dsts=[T.yq[b] for c in grp]))
             sent += 8
     g.remote_dma_fused(trs, local_sem=S.sent)
 
     if rank is not None:
+        lo = POS[host] * 8 * C
+        ol = (1 - POS[host]) * 8 * C
         g.dma_start(T.y[b * K:(b + 1) * K, :], T.il[:]).then_inc(S.own, 16)
-        g.sync.wait_ge(S.res, 8 * (W - 1))
-        g.sync.dma_start(T.y[0:b * K, :], T.yq[0:b]).then_inc(S.out, 16)
-        g.scalar.wait_ge(S.res, 8 * (W - 1))
-        g.scalar.dma_start(T.y[(b + 1) * K:, :], T.yq[b + 1:]).then_inc(S.out, 16)
+        g.sync.wait_ge(S.resoff, 8 * 8)
+        g.sync.dma_start(T.y[ol * K:(ol + 8) * K, :], T.yq[ol:ol + 8]).then_inc(S.out, 16)
+        g.scalar.wait_ge(S.resin, 8 * 7)
+        g.scalar.dma_start(T.y[lo * K:b * K, :], T.yq[lo:b]).then_inc(S.out, 16)
+        g.scalar.dma_start(T.y[(b + 1) * K:(lo + 8) * K, :], T.yq[b + 1:lo + 8]).then_inc(S.out, 16)
         g.wait_ge(S.own, 16)
-        g.wait_ge(S.out, 32)
+        g.wait_ge(S.out, 48)
     g.wait_ge(S.sent, sent)

from concourse.bass import DstId, RemoteDMATransfer

CHIPS = [6]
C = len(CHIPS)
W = 16 * C
K = 128 // W
M = K // 2

SCRATCH = {
    "xs": ("dram", [W, 128, M], "float32"),
    "inp": ("dram", [8, 128, M], "float32"),
    "il": ("dram", [128, 8 * M], "float32"),
    "yq": ("dram", [W, 128, 8 * M], "float32"),
}
SEMAPHORES = ["load", "near", "far", "wove", "resin", "resoff", "own", "out", "sent"]

POS = {0: 0, 3: 0, 1: 1, 2: 1}
HOST_AT = {(0, 0): 0, (0, 1): 1, (1, 0): 3, (1, 1): 2}


def worker_core(rack, b):
    pos, rest = divmod(b, 8 * C)
    ci, d = divmod(rest, 8)
    return HOST_AT[(rack, pos)] * 128 + CHIPS[ci] * 8 + d


def rank_program(g, core, T, topo):
    host, chip, d = topo.host(core), topo.chip(core), core % 8
    if chip not in CHIPS:
        return
    rack = topo.rack(host)
    rank = T.rank_of(core)
    b = (POS[host] * C + CHIPS.index(chip)) * 8 + d
    S = T.sem
    sent = 0

    def did(dst):
        rid, pid = topo.addr(dst, core)
        return DstId(rid=rid, pnc=pid)

    def on_chip(dst):
        return dst // 8 == core // 8

    if rank is not None:
        g.sync.dma_start(T.xs[:], T.x[:]).then_inc(S.load, 16)
        g.wait_ge(S.load, 16)
        near_in = [w for w in range(W) if on_chip(worker_core(rack, w)) and w != b]
        near_off = [w for w in range(W) if not on_chip(worker_core(rack, w))]
        while near_in or near_off:
            trs = []
            for e in range(8):
                if near_off:
                    w = near_off.pop(0)
                    trs.append(RemoteDMATransfer(dst_ids=[did(worker_core(rack, w))], dma_engine_mask=1 << e,
                                                 remote_sem=S.near, src=T.xs[w], dst=T.inp[rank]))
                if near_in:
                    w = near_in.pop(0)
                    trs.append(RemoteDMATransfer(dst_ids=[did(worker_core(rack, w))], dma_engine_mask=1 << (8 + e),
                                                 remote_sem=S.near, src=T.xs[w], dst=T.inp[rank]))
            g.remote_dma_fused(trs, local_sem=S.sent)
            sent += len(trs)

    def piece(r):
        return T.xs[b] if r == rank else T.inp[r]

    near = [4 * rack + q for q in range(4)]
    far = [4 * (1 - rack) + q for q in range(4)]

    g.wait_ge(S.near, 3 if rank is not None else 4)
    mate = did((3 - host) * 128 + chip * 8 + d)
    g.remote_dma_fused([RemoteDMATransfer(dst_ids=[mate], dma_engine_mask=3 << (2 * q), remote_sem=S.far,
                                          src=piece(r), dst=T.inp[r]) for q, r in enumerate(near)],
                       local_sem=S.sent)
    sent += 8

    for r in near:
        g.dma_start(T.il[:, r::8], piece(r), allow_slow_non_contiguous=True).then_inc(S.wove, 16)
    g.wait_ge(S.far, 8)
    for r in far:
        g.dma_start(T.il[:, r::8], piece(r), allow_slow_non_contiguous=True).then_inc(S.wove, 16)
    g.wait_ge(S.wove, 128)

    dsts = [T.cores[r] for r in near if r != rank]
    trs = []
    for mask, sem, grp in ((0x00FF, S.resoff, [c for c in dsts if not on_chip(c)]),
                           (0xFF00, S.resin, [c for c in dsts if on_chip(c)])):
        if grp:
            trs.append(RemoteDMATransfer(dst_ids=[did(c) for c in grp], dma_engine_mask=mask, remote_sem=sem,
                                         srcs=[T.il[:]], dsts=[T.yq[b] for c in grp]))
            sent += 8
    g.remote_dma_fused(trs, local_sem=S.sent)

    if rank is not None:
        lo = POS[host] * 8 * C
        ol = (1 - POS[host]) * 8 * C
        g.dma_start(T.y[b * K:(b + 1) * K, :], T.il[:]).then_inc(S.own, 16)
        g.sync.wait_ge(S.resoff, 8 * 8)
        g.sync.dma_start(T.y[ol * K:(ol + 8) * K, :], T.yq[ol:ol + 8]).then_inc(S.out, 16)
        g.scalar.wait_ge(S.resin, 8 * 7)
        g.scalar.dma_start(T.y[lo * K:b * K, :], T.yq[lo:b]).then_inc(S.out, 16)
        g.scalar.dma_start(T.y[(b + 1) * K:(lo + 8) * K, :], T.yq[b + 1:lo + 8]).then_inc(S.out, 16)
        g.wait_ge(S.own, 16)
        g.wait_ge(S.out, 48)
    g.wait_ge(S.sent, sent)
